import numpy as np
import ml_dtypes


def mxq(x, axis, fmt="e4m3"):
    dtype, down = {"e4m3": (ml_dtypes.float8_e4m3fn, 7), "e5m2": (ml_dtypes.float8_e5m2, 14)}[fmt]
    v = np.moveaxis(np.asarray(x, np.float32).astype(ml_dtypes.bfloat16).astype(np.float64), axis, -1)
    blocks = v.reshape(v.shape[:-1] + (-1, 32))
    amax = np.abs(blocks).max(-1, keepdims=True)
    byte = np.maximum(np.where(amax > 0, np.frexp(amax)[1] - 1 + 127, 0) - down, 1)
    scale = np.exp2(byte - 127.0)
    codes = (blocks / scale).astype(np.float32).astype(dtype).astype(np.float64)
    return np.moveaxis((codes * scale).reshape(v.shape), -1, axis)


WIDE = False


def mx_kscale(k):
    if not WIDE:
        return np.ones(k)
    levels = np.array([10, -10, 5, -5, 0])
    if k % 512:
        return np.exp2(np.random.permutation(np.resize(levels, k // 32))).repeat(32)
    a = np.empty((k // 512, 16))
    for p in range(k // 512):
        a[p, :8] = np.random.permutation(np.resize(levels, 8))
        for g in range(8):
            far = levels[np.abs(levels - a[p, g]) >= 10]
            a[p, g + 8] = far[np.random.randint(len(far))]
    return np.exp2(a.ravel()).repeat(32)


def f64(x):
    return np.asarray(x).astype(np.float64)


E2M1 = np.array([0.0, 0.5, 1.0, 1.5, 2.0, 3.0, 4.0, 6.0, -0.0, -0.5, -1.0, -1.5, -2.0, -3.0, -4.0, -6.0])


def pack_weight(w, fmt):
    k, n = w.shape
    w = f64(np.asarray(w, np.float32).astype(ml_dtypes.bfloat16)).reshape(k // 32, 32, n)
    amax = np.abs(w).max(1)
    if fmt == "e4m3":
        byte = np.frexp(amax)[1] - 1 + 127 - 7
    else:
        mant, ex = np.frexp(amax / 6.0)
        byte = np.where(mant > 0.5, ex, ex - 1) + 127
    byte = np.clip(np.where(amax > 0, byte, 1), 1, 254)
    scaled = (w * np.exp2(127.0 - byte)[:, None, :]).reshape(k, n).astype(np.float32)
    by_word = np.ascontiguousarray(scaled.reshape(k // 512, 128, 4, n).transpose(0, 1, 3, 2))
    if fmt == "e4m3":
        words = by_word.astype(ml_dtypes.float8_e4m3fn).view(np.uint8)
    else:
        c = by_word.astype(ml_dtypes.float4_e2m1fn).view(np.uint8) & 0xF
        words = (c[..., 0::2] | (c[..., 1::2] << 4)).reshape(k // 512, 128, 2 * n)
    return np.ascontiguousarray(words), np.ascontiguousarray(byte.astype(np.uint8).reshape(k // 512, 16, n))


def unpack_weight(words, scales, fmt):
    g, _, n = scales.shape
    words = np.ascontiguousarray(words).reshape(g, 128, n, -1)
    if fmt == "e4m3":
        vals = words.view(ml_dtypes.float8_e4m3fn).astype(np.float64)
    else:
        nib = np.empty((g, 128, n, 4), np.uint8)
        nib[..., 0::2] = words & 0xF
        nib[..., 1::2] = words >> 4
        vals = E2M1[nib]
    vals = vals * np.repeat(np.exp2(scales.astype(np.float64) - 127.0), 8, axis=1)[..., None]
    return vals.transpose(0, 1, 3, 2).reshape(g * 512, n)


K, L, M, T = 2048, 1024, 512, 1536


def setup_inputs():
    n = np.random.standard_normal
    s1 = mx_kscale(K)[:, None]
    s2 = mx_kscale(L)[:, None]
    p_wx = pack_weight(n((K, M)) / np.sqrt(K) / s1, "e2m1")
    p_wc = pack_weight(n((L, M)) / np.sqrt(L) / s2, "e4m3")
    return {
        "x": (n((K, T)) * s1).astype(np.float32),
        "c": (n((L, T)) * s2).astype(np.float32),
        "wx_words": p_wx[0],
        "wx_scales": p_wx[1],
        "wc_words": p_wc[0],
        "wc_scales": p_wc[1],
    }


def reference(x, c, wx_words, wx_scales, wc_words, wc_scales):
    x_ = mxq(f64(x), 0, "e4m3")
    c_ = mxq(f64(c), 0, "e4m3")
    wx_ = unpack_weight(wx_words, wx_scales, "e2m1")
    wc_ = unpack_weight(wc_words, wc_scales, "e4m3")
    y = x_.T @ wx_ + c_.T @ wc_
    return y

@@ -1,0 +1,167 @@
+from contextlib import ExitStack
+
+import concourse.mybir as mybir
+
+K, L, T, N = 2048, 1024, 1536, 512
+FLOPS = 2 * (K + L) * T * N
+
+F32 = mybir.dt.float32
+BF16 = mybir.dt.bfloat16
+I32 = mybir.dt.int32
+U32 = mybir.dt.uint32
+U8 = mybir.dt.uint8
+FP8X4 = mybir.dt.float8_e4m3fn_x4
+FP4X4 = mybir.dt.float4_e2m1fn_x4
+
+P = 128
+PACK = 4
+K_PASS = P * PACK
+X_PASSES = K // K_PASS
+C_PASSES = L // K_PASS
+PASSES = X_PASSES + C_PASSES
+W = 512
+BLOCKS = T // W
+TILES = W // P
+V_COLS = 336
+
+
+def tile_mix_skip_tm_none_kernel(tc, x, c, wx_words, wx_scales, wc_words, wc_scales, out):
+    nc = tc.nc
+    with ExitStack() as ctx:
+        keep = ctx.enter_context(tc.tile_pool(name="keep", bufs=1))
+        stage = ctx.enter_context(tc.tile_pool(name="stage", bufs=4))
+        results = ctx.enter_context(tc.tile_pool(name="results", bufs=6))
+        psum = ctx.enter_context(tc.psum_pool(name="psum", bufs=1))
+        ctx.enter_context(tc.manual_schedule())
+
+        wx_sb = keep.tile([P, X_PASSES, 2 * N], U8, name="wx_sb", align_bytes=64)
+        wc_sb = keep.tile([P, C_PASSES, 4 * N], U8, name="wc_sb", align_bytes=64)
+        wx_planes = keep.tile([P, X_PASSES * N], U8, name="wx_planes", align_bytes=64)
+        wc_planes = keep.tile([P, C_PASSES * N], U8, name="wc_planes", align_bytes=64)
+
+        raw = {}
+
+        def load(g, first, blocks):
+            src = x if g < X_PASSES else c
+            a = g if g < X_PASSES else g - X_PASSES
+            tile = keep.tile([P, PACK, blocks * W], F32, name=f"raw_{g}_{first}", align_bytes=64)
+            rows = src[a * K_PASS : (a + 1) * K_PASS, first * W : (first + blocks) * W]
+            nc.sync.dma_start(out=tile[:], in_=rows.rearrange("(p j) t -> p j t", j=PACK))
+            for b in range(blocks):
+                raw[g, first + b] = tile[:, :, b * W : (b + 1) * W]
+
+        def load_planes(planes, scales, passes):
+            for q in range(4):
+                nc.sync.dma_start(
+                    out=planes[32 * q : 32 * q + 4, :].bitcast(I32).rearrange("r (g n) -> r g n", g=passes),
+                    in_=scales.bitcast(I32)[:, 4 * q : 4 * q + 4, :].rearrange("g r n -> r g n"),
+                )
+
+        nc.vector.memset(wx_planes[:].bitcast(I32), 0)
+        nc.vector.memset(wc_planes[:].bitcast(I32), 0)
+        load(0, 0, 3)
+        load_planes(wx_planes, wx_scales, X_PASSES)
+        nc.sync.dma_start(out=wx_sb[:], in_=wx_words.rearrange("g p n -> p g n"))
+        load(1, 0, 3)
+        load(2, 0, 3)
+        nc.sync.dma_start(out=wc_sb[:], in_=wc_words.rearrange("g p n i -> p g (n i)"))
+        load_planes(wc_planes, wc_scales, C_PASSES)
+        load(3, 0, 3)
+        load(4, 0, 1)
+        load(5, 0, 1)
+        load(4, 1, 2)
+        load(5, 1, 1)
+        load(5, 2, 1)
+
+        grouped = {}
+        codes = {}
+        planes_of = {}
+
+        def cast(g, b, v_cols):
+            tile = stage.tile([P, W, PACK], BF16, name="grouped", align_bytes=64)
+            grouped[g, b] = tile
+            src = raw[g, b].rearrange("p j (c i) -> p c j i", i=4)
+            dst = tile[:].rearrange("p (c i) j -> p c j i", i=4)
+            cut = v_cols // 4
+            if cut > 0:
+                nc.vector.tensor_copy(out=dst[:, :cut], in_=src[:, :cut])
+            if cut < W // 4:
+                nc.scalar.copy(out=dst[:, cut:], in_=src[:, cut:])
+
+        def quantise(g, b):
+            codes[g, b] = keep.tile([P, W], U32, name=f"codes_{g}_{b}", align_bytes=64)
+            planes_of[g, b] = keep.tile([P, W], U8, name=f"planes_{g}_{b}", align_bytes=64)
+            nc.vector.quantize_mx(
+                out=codes[g, b][:].bitcast(FP8X4),
+                scales=planes_of[g, b][:],
+                in_=grouped[g, b][:].rearrange("p t j -> p (t j)"),
+            )
+
+        acc = {}
+
+        def multiply(g, b, order=range(TILES)):
+            for j in order:
+                if g == 0:
+                    acc[b, j] = psum.tile([P, N], F32, name=f"bank_{(b % 2) * TILES + j}")
+                cols = slice(j * P, (j + 1) * P)
+                if g < X_PASSES:
+                    rhs = wx_sb[:, g, :].bitcast(FP4X4)
+                    rhs_scale = wx_planes[:, g * N : (g + 1) * N]
+                else:
+                    a = g - X_PASSES
+                    rhs = wc_sb[:, a, :].bitcast(FP8X4)
+                    rhs_scale = wc_planes[:, a * N : (a + 1) * N]
+                nc.tensor.matmul_mx(
+                    out=acc[b, j][:],
+                    lhsT=codes[g, b][:, cols].bitcast(FP8X4),
+                    lhsT_scale=planes_of[g, b][:, cols],
+                    rhs=rhs,
+                    rhs_scale=rhs_scale,
+                    start=(g == 0),
+                    stop=(g == PASSES - 1),
+                )
+
+        def finish(b):
+            for j in range(TILES):
+                result = results.tile([P, N], F32, name="result", align_bytes=64)
+                if j % 2 == 0:
+                    nc.scalar.copy(out=result[:], in_=acc[b, j][:])
+                else:
+                    nc.vector.tensor_copy(out=result[:], in_=acc[b, j][:])
+                t0 = b * W + j * P
+                nc.sync.dma_start(out=out[t0 : t0 + P, :], in_=result[:])
+
+        for g in range(X_PASSES):
+            cast(g, 0, W)
+            cast(g, 1, W)
+            cast(g, 2, 0)
+            for b in range(BLOCKS):
+                quantise(g, b)
+            multiply(g, 0)
+            multiply(g, 1)
+
+        cast(4, 0, V_COLS)
+        quantise(4, 0)
+        multiply(4, 0)
+        cast(5, 0, V_COLS)
+        quantise(5, 0)
+        multiply(5, 0)
+        finish(0)
+
+        for g in range(3):
+            multiply(g, 2)
+        cast(4, 1, V_COLS)
+        cast(4, 2, V_COLS)
+        quantise(4, 1)
+        quantise(4, 2)
+        multiply(4, 1)
+        multiply(3, 2)
+        cast(5, 1, V_COLS)
+        quantise(5, 1)
+        multiply(5, 1)
+        cast(5, 2, V_COLS)
+        quantise(5, 2)
+        finish(1)
+        multiply(4, 2)
+        multiply(5, 2)
+        finish(2)

@@ -22,7 +22,7 @@ PASSES = X_PASSES + C_PASSES
 W = 512
 BLOCKS = T // W
 TILES = W // P
-V_COLS = 336
+V_COLS = 264
 
 
 def tile_mix_skip_tm_none_kernel(tc, x, c, wx_words, wx_scales, wc_words, wc_scales, out):
@@ -37,131 +37,173 @@ def tile_mix_skip_tm_none_kernel(tc, x, c, wx_words, wx_scales, wc_words, wc_sca
         wx_sb = keep.tile([P, X_PASSES, 2 * N], U8, name="wx_sb", align_bytes=64)
         wc_sb = keep.tile([P, C_PASSES, 4 * N], U8, name="wc_sb", align_bytes=64)
         wx_planes = keep.tile([P, X_PASSES * N], U8, name="wx_planes", align_bytes=64)
-        wc_planes = keep.tile([P, C_PASSES * N], U8, name="wc_planes", align_bytes=64)
+        wc_planes = keep.tile([P, N], U8, name="wc_planes", align_bytes=64)
 
         raw = {}
 
-        def load(g, first, blocks):
+        def load(g, first, tiles):
             src = x if g < X_PASSES else c
             a = g if g < X_PASSES else g - X_PASSES
-            tile = keep.tile([P, PACK, blocks * W], F32, name=f"raw_{g}_{first}", align_bytes=64)
-            rows = src[a * K_PASS : (a + 1) * K_PASS, first * W : (first + blocks) * W]
+            tile = keep.tile([P, PACK, tiles * P], F32, name=f"raw_{g}_{first}", align_bytes=64)
+            rows = src[a * K_PASS : (a + 1) * K_PASS, first * P : (first + tiles) * P]
             nc.sync.dma_start(out=tile[:], in_=rows.rearrange("(p j) t -> p j t", j=PACK))
-            for b in range(blocks):
-                raw[g, first + b] = tile[:, :, b * W : (b + 1) * W]
-
-        def load_planes(planes, scales, passes):
-            for q in range(4):
-                nc.sync.dma_start(
-                    out=planes[32 * q : 32 * q + 4, :].bitcast(I32).rearrange("r (g n) -> r g n", g=passes),
-                    in_=scales.bitcast(I32)[:, 4 * q : 4 * q + 4, :].rearrange("g r n -> r g n"),
-                )
+            for i in range(tiles):
+                raw[g, first + i] = (tile, i * P)
 
         nc.vector.memset(wx_planes[:].bitcast(I32), 0)
         nc.vector.memset(wc_planes[:].bitcast(I32), 0)
-        load(0, 0, 3)
-        load_planes(wx_planes, wx_scales, X_PASSES)
+        load(0, 0, 12)
+        for q in range(4):
+            nc.gpsimd.dma_start(
+                out=wx_planes[32 * q : 32 * q + 4, :].bitcast(I32).rearrange("r (g n) -> r g n", g=X_PASSES),
+                in_=wx_scales.bitcast(I32)[:, 4 * q : 4 * q + 4, :].rearrange("g r n -> r g n"),
+            )
         nc.sync.dma_start(out=wx_sb[:], in_=wx_words.rearrange("g p n -> p g n"))
-        load(1, 0, 3)
-        load(2, 0, 3)
+        load(1, 0, 12)
+        load(2, 0, 12)
         nc.sync.dma_start(out=wc_sb[:], in_=wc_words.rearrange("g p n i -> p g (n i)"))
-        load_planes(wc_planes, wc_scales, C_PASSES)
-        load(3, 0, 3)
-        load(4, 0, 1)
-        load(5, 0, 1)
-        load(4, 1, 2)
-        load(5, 1, 1)
-        load(5, 2, 1)
+        for q in range(4):
+            nc.gpsimd.dma_start(
+                out=wc_planes[32 * q + 4 : 32 * q + 12, :].bitcast(I32),
+                in_=wc_scales.bitcast(I32)[:, 4 * q : 4 * q + 4, :],
+            )
+        load(3, 0, 12)
+        load(4, 0, 8)
+        load(5, 0, 4)
+        load(4, 8, 4)
+        load(5, 4, 4)
+        load(5, 8, 4)
 
         grouped = {}
         codes = {}
-        planes_of = {}
 
-        def cast(g, b, v_cols):
-            tile = stage.tile([P, W, PACK], BF16, name="grouped", align_bytes=64)
-            grouped[g, b] = tile
-            src = raw[g, b].rearrange("p j (c i) -> p c j i", i=4)
-            dst = tile[:].rearrange("p (c i) j -> p c j i", i=4)
+        def cast(g, first, tiles, v_cols):
+            unit = stage.tile([P, W, PACK], BF16, name="grouped", align_bytes=64)
+            grouped[g, first] = unit
+            tile, c0 = raw[g, first]
+            cols = tiles * P
+            src = tile[:, :, c0 : c0 + cols].rearrange("p j (c i) -> p c j i", i=4)
+            dst = unit[:, :cols, :].rearrange("p (c i) j -> p c j i", i=4)
             cut = v_cols // 4
-            if cut > 0:
-                nc.vector.tensor_copy(out=dst[:, :cut], in_=src[:, :cut])
-            if cut < W // 4:
-                nc.scalar.copy(out=dst[:, cut:], in_=src[:, cut:])
+            nc.vector.tensor_copy(out=dst[:, :cut], in_=src[:, :cut])
+            nc.scalar.copy(out=dst[:, cut:], in_=src[:, cut:])
 
-        def quantise(g, b):
-            codes[g, b] = keep.tile([P, W], U32, name=f"codes_{g}_{b}", align_bytes=64)
-            planes_of[g, b] = keep.tile([P, W], U8, name=f"planes_{g}_{b}", align_bytes=64)
+        def quantise(g, first, tiles):
+            cols = tiles * P
+            words = keep.tile([P, cols], U32, name=f"codes_{g}_{first}", align_bytes=64)
+            planes = keep.tile([P, cols], U8, name=f"planes_{g}_{first}", align_bytes=64)
             nc.vector.quantize_mx(
-                out=codes[g, b][:].bitcast(FP8X4),
-                scales=planes_of[g, b][:],
-                in_=grouped[g, b][:].rearrange("p t j -> p (t j)"),
+                out=words[:].bitcast(FP8X4),
+                scales=planes[:],
+                in_=grouped[g, first][:, :cols, :].rearrange("p t j -> p (t j)"),
             )
+            for i in range(tiles):
+                codes[g, first + i] = (words[:, i * P : (i + 1) * P], planes[:, i * P : (i + 1) * P])
 
         acc = {}
 
-        def multiply(g, b, order=range(TILES)):
-            for j in order:
+        def multiply(g, first, tiles):
+            for i in range(first, first + tiles):
                 if g == 0:
-                    acc[b, j] = psum.tile([P, N], F32, name=f"bank_{(b % 2) * TILES + j}")
-                cols = slice(j * P, (j + 1) * P)
+                    acc[i] = psum.tile([P, N], F32, name=f"bank_{i % 8}")
                 if g < X_PASSES:
                     rhs = wx_sb[:, g, :].bitcast(FP4X4)
                     rhs_scale = wx_planes[:, g * N : (g + 1) * N]
                 else:
                     a = g - X_PASSES
                     rhs = wc_sb[:, a, :].bitcast(FP8X4)
-                    rhs_scale = wc_planes[:, a * N : (a + 1) * N]
+                    rhs_scale = wc_planes[4 * a + 4 :, :]
+                words, planes = codes[g, i]
                 nc.tensor.matmul_mx(
-                    out=acc[b, j][:],
-                    lhsT=codes[g, b][:, cols].bitcast(FP8X4),
-                    lhsT_scale=planes_of[g, b][:, cols],
+                    out=acc[i][:],
+                    lhsT=words.bitcast(FP8X4),
+                    lhsT_scale=planes,
                     rhs=rhs,
                     rhs_scale=rhs_scale,
                     start=(g == 0),
                     stop=(g == PASSES - 1),
                 )
 
-        def finish(b):
-            for j in range(TILES):
-                result = results.tile([P, N], F32, name="result", align_bytes=64)
-                if j % 2 == 0:
-                    nc.scalar.copy(out=result[:], in_=acc[b, j][:])
-                else:
-                    nc.vector.tensor_copy(out=result[:], in_=acc[b, j][:])
-                t0 = b * W + j * P
-                nc.sync.dma_start(out=out[t0 : t0 + P, :], in_=result[:])
+        def finish(i, engine):
+            result = results.tile([P, N], F32, name="result", align_bytes=64)
+            if engine == "scalar":
+                nc.scalar.copy(out=result[:], in_=acc[i][:])
+            else:
+                nc.vector.tensor_copy(out=result[:], in_=acc[i][:])
+            nc.sync.dma_start(out=out[i * P : (i + 1) * P, :], in_=result[:])
 
-        for g in range(X_PASSES):
-            cast(g, 0, W)
-            cast(g, 1, W)
-            cast(g, 2, 0)
-            for b in range(BLOCKS):
-                quantise(g, b)
-            multiply(g, 0)
-            multiply(g, 1)
-
-        cast(4, 0, V_COLS)
-        quantise(4, 0)
-        multiply(4, 0)
-        cast(5, 0, V_COLS)
-        quantise(5, 0)
-        multiply(5, 0)
-        finish(0)
-
-        for g in range(3):
-            multiply(g, 2)
-        cast(4, 1, V_COLS)
-        cast(4, 2, V_COLS)
-        quantise(4, 1)
-        quantise(4, 2)
-        multiply(4, 1)
-        multiply(3, 2)
-        cast(5, 1, V_COLS)
-        quantise(5, 1)
-        multiply(5, 1)
-        cast(5, 2, V_COLS)
-        quantise(5, 2)
-        finish(1)
-        multiply(4, 2)
-        multiply(5, 2)
-        finish(2)
+        cast(0, 0, 4, 264)
+        cast(0, 4, 4, 264)
+        quantise(0, 0, 4)
+        cast(0, 8, 4, 264)
+        quantise(0, 4, 4)
+        quantise(0, 8, 4)
+        multiply(0, 0, 4)
+        multiply(0, 4, 4)
+        cast(1, 0, 4, 264)
+        cast(1, 4, 4, 264)
+        quantise(1, 0, 4)
+        cast(1, 8, 4, 264)
+        quantise(1, 4, 4)
+        quantise(1, 8, 4)
+        multiply(1, 0, 4)
+        multiply(1, 4, 4)
+        cast(2, 0, 4, 264)
+        cast(2, 4, 4, 264)
+        quantise(2, 0, 4)
+        cast(2, 8, 4, 264)
+        quantise(2, 4, 4)
+        quantise(2, 8, 4)
+        multiply(2, 0, 4)
+        multiply(2, 4, 4)
+        cast(3, 0, 4, 264)
+        cast(3, 4, 4, 264)
+        quantise(3, 0, 4)
+        multiply(3, 0, 4)
+        cast(3, 8, 4, 264)
+        quantise(3, 4, 4)
+        multiply(3, 4, 4)
+        quantise(3, 8, 4)
+        cast(4, 0, 4, 264)
+        cast(4, 4, 4, 264)
+        quantise(4, 0, 4)
+        multiply(4, 0, 4)
+        cast(5, 0, 2, 168)
+        quantise(4, 4, 4)
+        multiply(4, 4, 4)
+        cast(5, 2, 2, 168)
+        quantise(5, 0, 2)
+        multiply(5, 0, 2)
+        quantise(5, 2, 2)
+        multiply(5, 2, 2)
+        finish(0, "scalar")
+        finish(1, "vector")
+        finish(2, "scalar")
+        finish(3, "vector")
+        multiply(0, 8, 4)
+        multiply(1, 8, 4)
+        multiply(2, 8, 4)
+        cast(4, 8, 4, 264)
+        cast(5, 4, 2, 168)
+        quantise(4, 8, 4)
+        cast(5, 6, 2, 168)
+        quantise(5, 4, 2)
+        multiply(5, 4, 2)
+        quantise(5, 6, 2)
+        multiply(5, 6, 2)
+        finish(4, "scalar")
+        finish(5, "vector")
+        multiply(3, 8, 4)
+        multiply(4, 8, 4)
+        finish(6, "scalar")
+        cast(5, 8, 2, 168)
+        cast(5, 10, 2, 168)
+        finish(7, "vector")
+        quantise(5, 8, 2)
+        multiply(5, 8, 2)
+        quantise(5, 10, 2)
+        multiply(5, 10, 2)
+        finish(8, "scalar")
+        finish(9, "vector")
+        finish(10, "scalar")
+        finish(11, "vector")

@@ -54,7 +54,7 @@ def tile_mix_skip_tm_none_kernel(tc, x, c, wx_words, wx_scales, wc_words, wc_sca
         nc.vector.memset(wc_planes[:].bitcast(I32), 0)
         load(0, 0, 12)
         for q in range(4):
-            nc.gpsimd.dma_start(
+            nc.sync.dma_start(
                 out=wx_planes[32 * q : 32 * q + 4, :].bitcast(I32).rearrange("r (g n) -> r g n", g=X_PASSES),
                 in_=wx_scales.bitcast(I32)[:, 4 * q : 4 * q + 4, :].rearrange("g r n -> r g n"),
             )
@@ -63,7 +63,7 @@ def tile_mix_skip_tm_none_kernel(tc, x, c, wx_words, wx_scales, wc_words, wc_sca
         load(2, 0, 12)
         nc.sync.dma_start(out=wc_sb[:], in_=wc_words.rearrange("g p n i -> p g (n i)"))
         for q in range(4):
-            nc.gpsimd.dma_start(
+            nc.sync.dma_start(
                 out=wc_planes[32 * q + 4 : 32 * q + 12, :].bitcast(I32),
                 in_=wc_scales.bitcast(I32)[:, 4 * q : 4 * q + 4, :],
             )
@@ -85,8 +85,10 @@ def tile_mix_skip_tm_none_kernel(tc, x, c, wx_words, wx_scales, wc_words, wc_sca
             src = tile[:, :, c0 : c0 + cols].rearrange("p j (c i) -> p c j i", i=4)
             dst = unit[:, :cols, :].rearrange("p (c i) j -> p c j i", i=4)
             cut = v_cols // 4
-            nc.vector.tensor_copy(out=dst[:, :cut], in_=src[:, :cut])
-            nc.scalar.copy(out=dst[:, cut:], in_=src[:, cut:])
+            if cut > 0:
+                nc.vector.tensor_copy(out=dst[:, :cut], in_=src[:, :cut])
+            if v_cols < cols:
+                nc.scalar.copy(out=dst[:, cut:], in_=src[:, cut:])
 
         def quantise(g, first, tiles):
             cols = tiles * P
@@ -156,54 +158,54 @@ def tile_mix_skip_tm_none_kernel(tc, x, c, wx_words, wx_scales, wc_words, wc_sca
         quantise(2, 8, 4)
         multiply(2, 0, 4)
         multiply(2, 4, 4)
-        cast(3, 0, 4, 264)
-        cast(3, 4, 4, 264)
+        cast(3, 0, 4, 320)
+        cast(3, 4, 4, 320)
         quantise(3, 0, 4)
         multiply(3, 0, 4)
-        cast(3, 8, 4, 264)
+        cast(3, 8, 4, 320)
         quantise(3, 4, 4)
         multiply(3, 4, 4)
         quantise(3, 8, 4)
-        cast(4, 0, 4, 264)
-        cast(4, 4, 4, 264)
+        cast(4, 0, 4, 320)
+        cast(4, 4, 4, 192)
         quantise(4, 0, 4)
-        multiply(4, 0, 4)
-        cast(5, 0, 2, 168)
         quantise(4, 4, 4)
+        multiply(4, 0, 4)
         multiply(4, 4, 4)
-        cast(5, 2, 2, 168)
+        cast(5, 0, 2, 128)
+        cast(5, 2, 2, 128)
         quantise(5, 0, 2)
         multiply(5, 0, 2)
         quantise(5, 2, 2)
         multiply(5, 2, 2)
         finish(0, "scalar")
-        finish(1, "vector")
         finish(2, "scalar")
+        finish(1, "vector")
         finish(3, "vector")
-        multiply(0, 8, 4)
-        multiply(1, 8, 4)
-        multiply(2, 8, 4)
-        cast(4, 8, 4, 264)
-        cast(5, 4, 2, 168)
-        quantise(4, 8, 4)
-        cast(5, 6, 2, 168)
+        cast(4, 8, 4, 64)
+        cast(5, 4, 2, 256)
         quantise(5, 4, 2)
-        multiply(5, 4, 2)
+        multiply(0, 8, 4)
+        multiply(2, 8, 4)
+        cast(5, 6, 2, 256)
+        quantise(4, 8, 4)
+        multiply(1, 8, 4)
         quantise(5, 6, 2)
-        multiply(5, 6, 2)
+        multiply(5, 4, 2)
+        cast(5, 8, 2, 256)
         finish(4, "scalar")
-        finish(5, "vector")
-        multiply(3, 8, 4)
-        multiply(4, 8, 4)
-        finish(6, "scalar")
-        cast(5, 8, 2, 168)
-        cast(5, 10, 2, 168)
-        finish(7, "vector")
         quantise(5, 8, 2)
+        multiply(3, 8, 4)
+        cast(5, 10, 2, 256)
+        multiply(5, 6, 2)
+        multiply(4, 8, 4)
+        finish(5, "scalar")
+        finish(6, "scalar")
         multiply(5, 8, 2)
         quantise(5, 10, 2)
+        finish(7, "scalar")
+        finish(8, "vector")
+        finish(9, "scalar")
         multiply(5, 10, 2)
-        finish(8, "scalar")
-        finish(9, "vector")
-        finish(10, "scalar")
+        finish(10, "vector")
         finish(11, "vector")

@@ -37,7 +37,7 @@ def tile_mix_skip_tm_none_kernel(tc, x, c, wx_words, wx_scales, wc_words, wc_sca
         wx_sb = keep.tile([P, X_PASSES, 2 * N], U8, name="wx_sb", align_bytes=64)
         wc_sb = keep.tile([P, C_PASSES, 4 * N], U8, name="wc_sb", align_bytes=64)
         wx_planes = keep.tile([P, X_PASSES * N], U8, name="wx_planes", align_bytes=64)
-        wc_planes = keep.tile([P, N], U8, name="wc_planes", align_bytes=64)
+        wc_planes = keep.tile([P, C_PASSES * N], U8, name="wc_planes", align_bytes=64)
 
         raw = {}
 
@@ -64,14 +64,15 @@ def tile_mix_skip_tm_none_kernel(tc, x, c, wx_words, wx_scales, wc_words, wc_sca
         nc.sync.dma_start(out=wc_sb[:], in_=wc_words.rearrange("g p n i -> p g (n i)"))
         for q in range(4):
             nc.sync.dma_start(
-                out=wc_planes[32 * q + 4 : 32 * q + 12, :].bitcast(I32),
-                in_=wc_scales.bitcast(I32)[:, 4 * q : 4 * q + 4, :],
+                out=wc_planes[32 * q : 32 * q + 4, :].bitcast(I32).rearrange("r (g n) -> r g n", g=C_PASSES),
+                in_=wc_scales.bitcast(I32)[:, 4 * q : 4 * q + 4, :].rearrange("g r n -> r g n"),
             )
         load(3, 0, 12)
-        load(4, 0, 8)
+        load(4, 0, 4)
         load(5, 0, 4)
-        load(4, 8, 4)
+        load(4, 4, 4)
         load(5, 4, 4)
+        load(4, 8, 4)
         load(5, 8, 4)
 
         grouped = {}
@@ -114,7 +115,7 @@ def tile_mix_skip_tm_none_kernel(tc, x, c, wx_words, wx_scales, wc_words, wc_sca
                 else:
                     a = g - X_PASSES
                     rhs = wc_sb[:, a, :].bitcast(FP8X4)
-                    rhs_scale = wc_planes[4 * a + 4 :, :]
+                    rhs_scale = wc_planes[:, a * N : (a + 1) * N]
                 words, planes = codes[g, i]
                 nc.tensor.matmul_mx(
                     out=acc[i][:],
@@ -158,54 +159,52 @@ def tile_mix_skip_tm_none_kernel(tc, x, c, wx_words, wx_scales, wc_words, wc_sca
         quantise(2, 8, 4)
         multiply(2, 0, 4)
         multiply(2, 4, 4)
-        cast(3, 0, 4, 320)
-        cast(3, 4, 4, 320)
+        cast(3, 0, 4, 264)
+        cast(3, 4, 4, 264)
         quantise(3, 0, 4)
-        multiply(3, 0, 4)
-        cast(3, 8, 4, 320)
+        cast(4, 0, 4, 264)
         quantise(3, 4, 4)
+        multiply(3, 0, 4)
         multiply(3, 4, 4)
-        quantise(3, 8, 4)
-        cast(4, 0, 4, 320)
-        cast(4, 4, 4, 192)
         quantise(4, 0, 4)
-        quantise(4, 4, 4)
-        multiply(4, 0, 4)
-        multiply(4, 4, 4)
         cast(5, 0, 2, 128)
         cast(5, 2, 2, 128)
+        cast(3, 8, 4, 264)
         quantise(5, 0, 2)
-        multiply(5, 0, 2)
         quantise(5, 2, 2)
-        multiply(5, 2, 2)
-        finish(0, "scalar")
-        finish(2, "scalar")
-        finish(1, "vector")
-        finish(3, "vector")
-        cast(4, 8, 4, 64)
-        cast(5, 4, 2, 256)
+        multiply(4, 0, 4)
+        multiply(5, 0, 4)
+        finish(0, "vector")
+        finish(1, "scalar")
+        finish(2, "vector")
+        finish(3, "scalar")
+        cast(4, 4, 4, 264)
+        quantise(3, 8, 4)
+        cast(5, 4, 2, 128)
+        quantise(4, 4, 4)
+        cast(5, 6, 2, 128)
         quantise(5, 4, 2)
-        multiply(0, 8, 4)
-        multiply(2, 8, 4)
-        cast(5, 6, 2, 256)
-        quantise(4, 8, 4)
-        multiply(1, 8, 4)
         quantise(5, 6, 2)
+        multiply(0, 8, 4)
+        multiply(1, 8, 4)
+        multiply(2, 8, 4)
+        multiply(4, 4, 4)
         multiply(5, 4, 2)
-        cast(5, 8, 2, 256)
-        finish(4, "scalar")
-        quantise(5, 8, 2)
         multiply(3, 8, 4)
-        cast(5, 10, 2, 256)
-        multiply(5, 6, 2)
-        multiply(4, 8, 4)
+        cast(4, 8, 4, 264)
+        finish(4, "vector")
         finish(5, "scalar")
-        finish(6, "scalar")
-        multiply(5, 8, 2)
+        quantise(4, 8, 4)
+        cast(5, 8, 2, 224)
+        quantise(5, 8, 2)
+        cast(5, 10, 2, 224)
         quantise(5, 10, 2)
+        multiply(5, 6, 2)
+        finish(6, "scalar")
         finish(7, "scalar")
-        finish(8, "vector")
-        finish(9, "scalar")
-        multiply(5, 10, 2)
+        multiply(4, 8, 4)
+        multiply(5, 8, 4)
+        finish(8, "scalar")
+        finish(9, "vector")
         finish(10, "vector")
-        finish(11, "vector")
+        finish(11, "scalar")

from contextlib import ExitStack

import concourse.mybir as mybir

K, L, T, N = 2048, 1024, 1536, 512
FLOPS = 2 * (K + L) * T * N

F32 = mybir.dt.float32
BF16 = mybir.dt.bfloat16
I32 = mybir.dt.int32
U32 = mybir.dt.uint32
U8 = mybir.dt.uint8
FP8X4 = mybir.dt.float8_e4m3fn_x4
FP4X4 = mybir.dt.float4_e2m1fn_x4

P = 128
PACK = 4
K_PASS = P * PACK
X_PASSES = K // K_PASS
C_PASSES = L // K_PASS
PASSES = X_PASSES + C_PASSES
W = 512
BLOCKS = T // W
TILES = W // P
V_COLS = 264


def tile_mix_skip_tm_none_kernel(tc, x, c, wx_words, wx_scales, wc_words, wc_scales, out):
    nc = tc.nc
    with ExitStack() as ctx:
        keep = ctx.enter_context(tc.tile_pool(name="keep", bufs=1))
        stage = ctx.enter_context(tc.tile_pool(name="stage", bufs=4))
        results = ctx.enter_context(tc.tile_pool(name="results", bufs=6))
        psum = ctx.enter_context(tc.psum_pool(name="psum", bufs=1))
        ctx.enter_context(tc.manual_schedule())

        wx_sb = keep.tile([P, X_PASSES, 2 * N], U8, name="wx_sb", align_bytes=64)
        wc_sb = keep.tile([P, C_PASSES, 4 * N], U8, name="wc_sb", align_bytes=64)
        wx_planes = keep.tile([P, X_PASSES * N], U8, name="wx_planes", align_bytes=64)
        wc_planes = keep.tile([P, C_PASSES * N], U8, name="wc_planes", align_bytes=64)

        raw = {}

        def load(g, first, tiles):
            src = x if g < X_PASSES else c
            a = g if g < X_PASSES else g - X_PASSES
            tile = keep.tile([P, PACK, tiles * P], F32, name=f"raw_{g}_{first}", align_bytes=64)
            rows = src[a * K_PASS : (a + 1) * K_PASS, first * P : (first + tiles) * P]
            nc.sync.dma_start(out=tile[:], in_=rows.rearrange("(p j) t -> p j t", j=PACK))
            for i in range(tiles):
                raw[g, first + i] = (tile, i * P)

        nc.vector.memset(wx_planes[:].bitcast(I32), 0)
        nc.vector.memset(wc_planes[:].bitcast(I32), 0)
        load(0, 0, 12)
        for q in range(4):
            nc.sync.dma_start(
                out=wx_planes[32 * q : 32 * q + 4, :].bitcast(I32).rearrange("r (g n) -> r g n", g=X_PASSES),
                in_=wx_scales.bitcast(I32)[:, 4 * q : 4 * q + 4, :].rearrange("g r n -> r g n"),
            )
        nc.sync.dma_start(out=wx_sb[:], in_=wx_words.rearrange("g p n -> p g n"))
        load(1, 0, 12)
        load(2, 0, 12)
        nc.sync.dma_start(out=wc_sb[:], in_=wc_words.rearrange("g p n i -> p g (n i)"))
        for q in range(4):
            nc.sync.dma_start(
                out=wc_planes[32 * q : 32 * q + 4, :].bitcast(I32).rearrange("r (g n) -> r g n", g=C_PASSES),
                in_=wc_scales.bitcast(I32)[:, 4 * q : 4 * q + 4, :].rearrange("g r n -> r g n"),
            )
        load(3, 0, 12)
        load(4, 0, 4)
        load(5, 0, 4)
        load(4, 4, 4)
        load(5, 4, 4)
        load(4, 8, 4)
        load(5, 8, 4)

        grouped = {}
        codes = {}

        def cast(g, first, tiles, v_cols):
            unit = stage.tile([P, W, PACK], BF16, name="grouped", align_bytes=64)
            grouped[g, first] = unit
            tile, c0 = raw[g, first]
            cols = tiles * P
            src = tile[:, :, c0 : c0 + cols].rearrange("p j (c i) -> p c j i", i=4)
            dst = unit[:, :cols, :].rearrange("p (c i) j -> p c j i", i=4)
            cut = v_cols // 4
            if cut > 0:
                nc.vector.tensor_copy(out=dst[:, :cut], in_=src[:, :cut])
            if v_cols < cols:
                nc.scalar.copy(out=dst[:, cut:], in_=src[:, cut:])

        def quantise(g, first, tiles):
            cols = tiles * P
            words = keep.tile([P, cols], U32, name=f"codes_{g}_{first}", align_bytes=64)
            planes = keep.tile([P, cols], U8, name=f"planes_{g}_{first}", align_bytes=64)
            nc.vector.quantize_mx(
                out=words[:].bitcast(FP8X4),
                scales=planes[:],
                in_=grouped[g, first][:, :cols, :].rearrange("p t j -> p (t j)"),
            )
            for i in range(tiles):
                codes[g, first + i] = (words[:, i * P : (i + 1) * P], planes[:, i * P : (i + 1) * P])

        acc = {}

        def multiply(g, first, tiles):
            for i in range(first, first + tiles):
                if g == 0:
                    acc[i] = psum.tile([P, N], F32, name=f"bank_{i % 8}")
                if g < X_PASSES:
                    rhs = wx_sb[:, g, :].bitcast(FP4X4)
                    rhs_scale = wx_planes[:, g * N : (g + 1) * N]
                else:
                    a = g - X_PASSES
                    rhs = wc_sb[:, a, :].bitcast(FP8X4)
                    rhs_scale = wc_planes[:, a * N : (a + 1) * N]
                words, planes = codes[g, i]
                nc.tensor.matmul_mx(
                    out=acc[i][:],
                    lhsT=words.bitcast(FP8X4),
                    lhsT_scale=planes,
                    rhs=rhs,
                    rhs_scale=rhs_scale,
                    start=(g == 0),
                    stop=(g == PASSES - 1),
                )

        def finish(i, engine):
            result = results.tile([P, N], F32, name="result", align_bytes=64)
            if engine == "scalar":
                nc.scalar.copy(out=result[:], in_=acc[i][:])
            else:
                nc.vector.tensor_copy(out=result[:], in_=acc[i][:])
            nc.sync.dma_start(out=out[i * P : (i + 1) * P, :], in_=result[:])

        cast(0, 0, 4, 264)
        cast(0, 4, 4, 264)
        quantise(0, 0, 4)
        cast(0, 8, 4, 264)
        quantise(0, 4, 4)
        quantise(0, 8, 4)
        multiply(0, 0, 4)
        multiply(0, 4, 4)
        cast(1, 0, 4, 264)
        cast(1, 4, 4, 264)
        quantise(1, 0, 4)
        cast(1, 8, 4, 264)
        quantise(1, 4, 4)
        quantise(1, 8, 4)
        multiply(1, 0, 4)
        multiply(1, 4, 4)
        cast(2, 0, 4, 264)
        cast(2, 4, 4, 264)
        quantise(2, 0, 4)
        cast(2, 8, 4, 264)
        quantise(2, 4, 4)
        quantise(2, 8, 4)
        multiply(2, 0, 4)
        multiply(2, 4, 4)
        cast(3, 0, 4, 264)
        cast(3, 4, 4, 264)
        quantise(3, 0, 4)
        cast(4, 0, 4, 264)
        quantise(3, 4, 4)
        multiply(3, 0, 4)
        multiply(3, 4, 4)
        quantise(4, 0, 4)
        cast(5, 0, 2, 128)
        cast(5, 2, 2, 128)
        cast(3, 8, 4, 264)
        quantise(5, 0, 2)
        quantise(5, 2, 2)
        multiply(4, 0, 4)
        multiply(5, 0, 4)
        finish(0, "vector")
        finish(1, "scalar")
        finish(2, "vector")
        finish(3, "scalar")
        cast(4, 4, 4, 264)
        quantise(3, 8, 4)
        cast(5, 4, 2, 128)
        quantise(4, 4, 4)
        cast(5, 6, 2, 128)
        quantise(5, 4, 2)
        quantise(5, 6, 2)
        multiply(0, 8, 4)
        multiply(1, 8, 4)
        multiply(2, 8, 4)
        multiply(4, 4, 4)
        multiply(5, 4, 2)
        multiply(3, 8, 4)
        cast(4, 8, 4, 264)
        finish(4, "vector")
        finish(5, "scalar")
        quantise(4, 8, 4)
        cast(5, 8, 2, 224)
        quantise(5, 8, 2)
        cast(5, 10, 2, 224)
        quantise(5, 10, 2)
        multiply(5, 6, 2)
        finish(6, "scalar")
        finish(7, "scalar")
        multiply(4, 8, 4)
        multiply(5, 8, 4)
        finish(8, "scalar")
        finish(9, "vector")
        finish(10, "vector")
        finish(11, "scalar")
